import numpy as np
import ml_dtypes


def mxq(x, axis, fmt="e4m3"):
    dtype, down = {"e4m3": (ml_dtypes.float8_e4m3fn, 7), "e5m2": (ml_dtypes.float8_e5m2, 14)}[fmt]
    v = np.moveaxis(np.asarray(x, np.float32).astype(ml_dtypes.bfloat16).astype(np.float64), axis, -1)
    blocks = v.reshape(v.shape[:-1] + (-1, 32))
    amax = np.abs(blocks).max(-1, keepdims=True)
    byte = np.maximum(np.where(amax > 0, np.frexp(amax)[1] - 1 + 127, 0) - down, 1)
    scale = np.exp2(byte - 127.0)
    codes = (blocks / scale).astype(np.float32).astype(dtype).astype(np.float64)
    return np.moveaxis((codes * scale).reshape(v.shape), -1, axis)


WIDE = False


def mx_kscale(k):
    if not WIDE:
        return np.ones(k)
    levels = np.array([10, -10, 5, -5, 0])
    if k % 512:
        return np.exp2(np.random.permutation(np.resize(levels, k // 32))).repeat(32)
    a = np.empty((k // 512, 16))
    for p in range(k // 512):
        a[p, :8] = np.random.permutation(np.resize(levels, 8))
        for g in range(8):
            far = levels[np.abs(levels - a[p, g]) >= 10]
            a[p, g + 8] = far[np.random.randint(len(far))]
    return np.exp2(a.ravel()).repeat(32)


def f64(x):
    return np.asarray(x).astype(np.float64)


def striped(idx):
    return np.tile(np.asarray(idx).reshape(-1, 16).T, (8, 1)).astype(np.uint16)


def unstriped(offs):
    return offs[:16].T.reshape(-1).astype(np.int64)


E2M1 = np.array([0.0, 0.5, 1.0, 1.5, 2.0, 3.0, 4.0, 6.0, -0.0, -0.5, -1.0, -1.5, -2.0, -3.0, -4.0, -6.0])


def pack_weight(w, fmt):
    k, n = w.shape
    w = f64(np.asarray(w, np.float32).astype(ml_dtypes.bfloat16)).reshape(k // 32, 32, n)
    amax = np.abs(w).max(1)
    if fmt == "e4m3":
        byte = np.frexp(amax)[1] - 1 + 127 - 7
    else:
        mant, ex = np.frexp(amax / 6.0)
        byte = np.where(mant > 0.5, ex, ex - 1) + 127
    byte = np.clip(np.where(amax > 0, byte, 1), 1, 254)
    scaled = (w * np.exp2(127.0 - byte)[:, None, :]).reshape(k, n).astype(np.float32)
    by_word = np.ascontiguousarray(scaled.reshape(k // 512, 128, 4, n).transpose(0, 1, 3, 2))
    if fmt == "e4m3":
        words = by_word.astype(ml_dtypes.float8_e4m3fn).view(np.uint8)
    else:
        c = by_word.astype(ml_dtypes.float4_e2m1fn).view(np.uint8) & 0xF
        words = (c[..., 0::2] | (c[..., 1::2] << 4)).reshape(k // 512, 128, 2 * n)
    return np.ascontiguousarray(words), np.ascontiguousarray(byte.astype(np.uint8).reshape(k // 512, 16, n))


def unpack_weight(words, scales, fmt):
    g, _, n = scales.shape
    words = np.ascontiguousarray(words).reshape(g, 128, n, -1)
    if fmt == "e4m3":
        vals = words.view(ml_dtypes.float8_e4m3fn).astype(np.float64)
    else:
        nib = np.empty((g, 128, n, 4), np.uint8)
        nib[..., 0::2] = words & 0xF
        nib[..., 1::2] = words >> 4
        vals = E2M1[nib]
    vals = vals * np.repeat(np.exp2(scales.astype(np.float64) - 127.0), 8, axis=1)[..., None]
    return vals.transpose(0, 1, 3, 2).reshape(g * 512, n)


D, E, T, I, Q, G = 512, 512, 2048, 512, 128, 64


def setup_inputs():
    n = np.random.standard_normal
    idx = np.random.permutation(T)[:I]
    fd = mx_kscale(D)
    fe = mx_kscale(E)
    keysp = pack_weight(n((D, T)) / fd[:, None], "e2m1")
    valsp = pack_weight(n((E, T)) / fe[:, None], "e2m1")
    return {
        "query": (n((D, Q)) * 0.5 / np.sqrt(D) * fd[:, None]).astype(np.float32),
        "keys_words": keysp[0],
        "keys_scales": keysp[1],
        "gout": (n((E, Q)) * 1 / np.sqrt(E) * fe[:, None]).astype(np.float32),
        "vals_words": valsp[0],
        "vals_scales": valsp[1],
        "size": (np.random.uniform(0.5, 2.0, (1, I))).astype(np.float32),
        "old": (0.5 * n((Q, T))).astype(np.float32),
        "offs": striped(idx),
    }


def reference(query, keys_words, keys_scales, gout, vals_words, vals_scales, size, old, offs):
    idx = unstriped(offs)
    keysu = unpack_weight(keys_words, keys_scales, "e2m1")
    valsu = unpack_weight(vals_words, vals_scales, "e2m1")
    queryq = mxq(f64(query), 0, "e4m3")
    keysidxg = keysu[:, idx]
    a = queryq.T @ keysidxg
    p = np.exp(a)
    z = np.sum(p, axis=1, keepdims=True)
    p2 = np.square(p)
    s1 = p.reshape(Q, G, I // G).sum(axis=2)
    s2 = p2.reshape(Q, G, I // G).sum(axis=2)
    sh = s1 / s2 / z
    sr = np.repeat(sh, I // G, axis=1)
    goutq = mxq(f64(gout), 0, "e4m3")
    valsidxg = valsu[:, idx]
    c0 = goutq.T @ valsidxg
    dsr = c0 * f64(size) * p2
    dsh = dsr.reshape(Q, G, I // G).sum(axis=2)
    ds2 = dsh / z * s1 / np.square(s2) * (-1.0)
    r1 = np.repeat(ds2, I // G, axis=1)
    ds1 = dsh / z / s2
    r2 = np.repeat(ds1, I // G, axis=1)
    dp2 = c0 * f64(size) * sr + r1
    dz = np.sum(dsh * s1 / s2 / np.square(z) * (-1.0), axis=1, keepdims=True)
    dp = r2 + dp2 * p * 2.0 + dz
    da = dp * p
    gs = da * 512.0
    gf = np.zeros((Q, T))
    gf[:, idx] = gs
    y = f64(old) + gf
    return y

@@ -1,0 +1,160 @@
+from contextlib import ExitStack
+
+import concourse.mybir as mybir
+from concourse.masks import make_identity
+
+D, E, T, I, Q, G = 512, 512, 2048, 512, 128, 64
+FLOPS = 2 * 2 * 512 * Q * I
+
+F32 = mybir.dt.float32
+BF16 = mybir.dt.bfloat16
+I32 = mybir.dt.int32
+U32 = mybir.dt.uint32
+U16 = mybir.dt.uint16
+U8 = mybir.dt.uint8
+FP8X4 = mybir.dt.float8_e4m3fn_x4
+FP4X4 = mybir.dt.float4_e2m1fn_x4
+ACT = mybir.ActivationFunctionType
+ALU = mybir.AluOpType
+AX = mybir.AxisListType
+
+P = 128
+PACK = 4
+GS = I // G
+HALVES = 2
+OUT_CHUNKS = (256, 512, 512, 512, 256)
+
+
+def tile_attend_bshareofshare_s_kernel(tc, query, keys_words, keys_scales, gout, vals_words, vals_scales, size, old, offs, out):
+    nc = tc.nc
+    with ExitStack() as ctx:
+        sb = ctx.enter_context(tc.tile_pool(name="sb", bufs=1))
+        ps = ctx.enter_context(tc.psum_pool(name="ps", bufs=1))
+
+        offsets = sb.tile([P, I // 16], U16, name="offsets")
+        k_words = sb.tile([P, T], U16, name="k_words", align_bytes=64)
+        v_words = sb.tile([P, T], U16, name="v_words", align_bytes=64)
+        k_bytes = sb.tile([P, T], U8, name="k_bytes", align_bytes=64)
+        v_bytes = sb.tile([P, T], U8, name="v_bytes", align_bytes=64)
+        q_raw = sb.tile([P, PACK, Q], F32, name="q_raw", align_bytes=64)
+        g_raw = sb.tile([P, PACK, Q], F32, name="g_raw", align_bytes=64)
+        size_col = sb.tile([P, PACK], F32, name="size_col")
+        old_sb = sb.tile([P, T], F32, name="old_sb", align_bytes=64)
+        placed = sb.tile([P, T], F32, name="placed", align_bytes=64)
+        warm = sb.tile([P, 1], F32, name="warm")
+        warm_out = sb.tile([P, 1], F32, name="warm_out")
+        ident = sb.tile([P, P], F32, name="ident", align_bytes=64)
+
+        nc.vector.memset(k_bytes[:].bitcast(I32), 0)
+        nc.vector.memset(v_bytes[:].bitcast(I32), 0)
+        nc.vector.memset(warm[:], 0.0)
+        nc.gpsimd.dma_start(out=size_col[:], in_=size.rearrange("o (p t) -> p (o t)", t=PACK))
+        make_identity(nc, ident[:])
+        nc.gpsimd.memset(placed[:], 0.0)
+
+        def load_scale_rows(tile, scales):
+            for r in range(4):
+                nc.sync.dma_start(out=tile[r:P:32, :].bitcast(I32), in_=scales[0, r:16:4, :].bitcast(I32))
+
+        nc.sync.dma_start(offsets[:], offs)
+        nc.scalar.dma_start(out=k_words[:].bitcast(I32), in_=keys_words[0].bitcast(I32))
+        load_scale_rows(k_bytes, keys_scales)
+        nc.scalar.dma_start(out=q_raw[:], in_=query.rearrange("(p j) q -> p j q", j=PACK))
+        nc.scalar.dma_start(out=v_words[:].bitcast(I32), in_=vals_words[0].bitcast(I32))
+        nc.scalar.activation(warm_out[:], warm[:], ACT.Exp)
+        load_scale_rows(v_bytes, vals_scales)
+        nc.sync.dma_start(out=g_raw[:], in_=gout.rearrange("(p j) q -> p j q", j=PACK))
+        nc.sync.dma_start(out=old_sb[:], in_=old)
+
+        size_ps = ps.tile([P, PACK, P], F32, name="size_ps")
+        for t in range(PACK):
+            nc.tensor.transpose(size_ps[:, t, :], size_col[:, t:t + 1].to_broadcast([P, P]), ident[:])
+        size_row = sb.tile([P, P, PACK], F32, name="size_row", align_bytes=64)
+        nc.scalar.copy(size_row[:], size_ps[:].rearrange("q t p -> q p t"))
+        size_flat = size_row[:].rearrange("q p t -> q (p t)")
+
+        def product(raw, words, scale_bytes, name):
+            grouped = sb.tile([P, Q, PACK], BF16, name=name + "_grouped", align_bytes=64)
+            codes = sb.tile([P, Q], U32, name=name + "_codes", align_bytes=64)
+            scales = sb.tile([P, Q], U8, name=name + "_scales", align_bytes=64)
+            picked_words = sb.tile([P, I], U16, name=name + "_picked_words", align_bytes=64)
+            picked_bytes = sb.tile([P, I], U8, name=name + "_picked_bytes", align_bytes=64)
+            acc = ps.tile([P, I], F32, name=name + "_acc")
+            nc.scalar.copy(grouped[:], raw[:].rearrange("p j q -> p q j"))
+            nc.vector.tensor_copy(picked_words[:], words[:].indirect(offsets[:]))
+            nc.vector.quantize_mx(out=codes[:].bitcast(FP8X4), scales=scales[:], in_=grouped[:].rearrange("p q j -> p (q j)"))
+            nc.vector.tensor_copy(picked_bytes[:], scale_bytes[:].indirect(offsets[:]))
+            nc.tensor.matmul_mx(out=acc[:], lhsT=codes[:].bitcast(FP8X4), lhsT_scale=scales[:],
+                                rhs=picked_words[:].bitcast(FP4X4), rhs_scale=picked_bytes[:], start=True, stop=True)
+            return acc
+
+        a = product(q_raw, k_words, k_bytes, "a")
+
+        p = sb.tile([P, I], F32, name="p", align_bytes=64)
+        p2 = sb.tile([P, I], F32, name="p2", align_bytes=64)
+        s2z = sb.tile([P, G + 1], F32, name="s2z", align_bytes=64)
+        nc.scalar.activation(p2[:], a[:], ACT.Exp, scale=2.0)
+        nc.scalar.activation(p[:], a[:], ACT.Exp, accum_out=s2z[:, G:G + 1])
+
+        c0 = product(g_raw, v_words, v_bytes, "c")
+
+        def grp(ap):
+            return ap.rearrange("q (g j) -> q g j", j=GS)
+
+        def spread(ap, n):
+            return ap.unsqueeze(2).to_broadcast([P, n, GS])
+
+        s1 = sb.tile([P, G], F32, name="s1", align_bytes=64)
+        nc.vector.tensor_reduce(s2z[:, 0:G], grp(p2[:]), AX.X, ALU.add)
+        nc.vector.tensor_reduce(s1[:], grp(p[:]), AX.X, ALU.add)
+        root = sb.tile([P, G + 1], F32, name="root", align_bytes=64)
+        inv = sb.tile([P, G + 1], F32, name="inv", align_bytes=64)
+        nc.scalar.activation(root[:], s2z[:], ACT.Abs_reciprocal_sqrt)
+        nc.scalar.activation(inv[:], root[:], ACT.Square)
+        inv_s2 = inv[:, 0:G]
+        inv_z = inv[:, G:G + 1]
+
+        w = sb.tile([P, I], F32, name="w", align_bytes=64)
+        u = sb.tile([P, I], F32, name="u", align_bytes=64)
+        dsh = sb.tile([P, G], F32, name="dsh", align_bytes=64)
+        sh = sb.tile([P, G], F32, name="sh", align_bytes=64)
+        psh = sb.tile([P, I], F32, name="psh", align_bytes=64)
+        mean = sb.tile([P, G], F32, name="mean", align_bytes=64)
+        junk = sb.tile([P, G], F32, name="junk", align_bytes=64)
+        total = sb.tile([P, 1], F32, name="total")
+        lin = sb.tile([P, G], F32, name="lin", align_bytes=64)
+        y1 = sb.tile([P, I], F32, name="y1", align_bytes=64)
+        y2 = sb.tile([P, I], F32, name="y2", align_bytes=64)
+        y3 = sb.tile([P, I], F32, name="y3", align_bytes=64)
+
+        cols = [slice(h * I // HALVES, (h + 1) * I // HALVES) for h in range(HALVES)]
+        grps = [slice(h * G // HALVES, (h + 1) * G // HALVES) for h in range(HALVES)]
+        gh = G // HALVES
+
+        for c in cols:
+            nc.vector.tensor_tensor(w[:, c], c0[:, c], size_flat[:, c], ALU.mult)
+        for c in cols:
+            nc.vector.tensor_tensor(u[:, c], w[:, c], p2[:, c], ALU.mult)
+        nc.vector.scalar_tensor_tensor(sh[:], s1[:], inv_z, inv_s2, ALU.mult, ALU.mult)
+        for c, g in zip(cols, grps):
+            nc.vector.tensor_reduce(dsh[:, g], grp(u[:, c]), AX.X, ALU.add)
+        nc.vector.tensor_tensor(grp(psh[:]), grp(p[:]), spread(sh[:], G), ALU.mult)
+        nc.vector.tensor_tensor(mean[:], dsh[:], inv_s2, ALU.mult)
+        nc.vector.scalar_tensor_tensor(junk[:], dsh[:], -1.0, sh[:], ALU.mult, ALU.mult, accum_out=total[:])
+        for c, g in zip(cols, grps):
+            nc.vector.tensor_tensor(grp(y1[:, c]), grp(w[:, c]), spread(mean[:, g], gh), ALU.subtract)
+        nc.vector.tensor_scalar(lin[:], mean[:], total[:], inv_z, ALU.add, ALU.mult)
+        for c in cols:
+            nc.vector.scalar_tensor_tensor(y2[:, c], y1[:, c], 1024.0, psh[:, c], ALU.mult, ALU.mult)
+        for c, g in zip(cols, grps):
+            nc.vector.scalar_tensor_tensor(grp(y3[:, c]), spread(lin[:, g], gh), 512.0, grp(y2[:, c]), ALU.mult, ALU.add)
+        nc.vector.tensor_tensor(placed[:].indirect(offsets[:]), y3[:], p[:], ALU.mult)
+
+        start = 0
+        for n, width in enumerate(OUT_CHUNKS):
+            c = slice(start, start + width)
+            start = start + width
+            res = sb.tile([P, width], F32, name="res%d" % n, align_bytes=64)
+            nc.vector.tensor_tensor(res[:], old_sb[:, c], placed[:, c], ALU.add)
+            queue = nc.sync if n % 2 == 0 else nc.scalar
+            queue.dma_start(out=out[:, c], in_=res[:])

@@ -1,7 +1,6 @@
 from contextlib import ExitStack
 
 import concourse.mybir as mybir
-from concourse.masks import make_identity
 
 D, E, T, I, Q, G = 512, 512, 2048, 512, 128, 64
 FLOPS = 2 * 2 * 512 * Q * I
@@ -22,7 +21,7 @@ P = 128
 PACK = 4
 GS = I // G
 HALVES = 2
-OUT_CHUNKS = (256, 512, 512, 512, 256)
+OUT_CHUNKS = (256, 768, 768, 256)
 
 
 def tile_attend_bshareofshare_s_kernel(tc, query, keys_words, keys_scales, gout, vals_words, vals_scales, size, old, offs, out):
@@ -32,46 +31,33 @@ def tile_attend_bshareofshare_s_kernel(tc, query, keys_words, keys_scales, gout,
         ps = ctx.enter_context(tc.psum_pool(name="ps", bufs=1))
 
         offsets = sb.tile([P, I // 16], U16, name="offsets")
-        k_words = sb.tile([P, T], U16, name="k_words", align_bytes=64)
-        v_words = sb.tile([P, T], U16, name="v_words", align_bytes=64)
-        k_bytes = sb.tile([P, T], U8, name="k_bytes", align_bytes=64)
-        v_bytes = sb.tile([P, T], U8, name="v_bytes", align_bytes=64)
+        k_words = sb.tile([P, T], U16, name="k_words", tag="k_words", align_bytes=64)
+        v_words = sb.tile([P, T], U16, name="v_words", tag="v_words", align_bytes=64)
+        k_bytes = sb.tile([P, T], U8, name="k_bytes", tag="k_bytes", align_bytes=64)
+        v_bytes = sb.tile([P, T], U8, name="v_bytes", tag="v_bytes", align_bytes=64)
         q_raw = sb.tile([P, PACK, Q], F32, name="q_raw", align_bytes=64)
         g_raw = sb.tile([P, PACK, Q], F32, name="g_raw", align_bytes=64)
-        size_col = sb.tile([P, PACK], F32, name="size_col")
-        old_sb = sb.tile([P, T], F32, name="old_sb", align_bytes=64)
         placed = sb.tile([P, T], F32, name="placed", align_bytes=64)
         warm = sb.tile([P, 1], F32, name="warm")
         warm_out = sb.tile([P, 1], F32, name="warm_out")
-        ident = sb.tile([P, P], F32, name="ident", align_bytes=64)
 
         nc.vector.memset(k_bytes[:].bitcast(I32), 0)
         nc.vector.memset(v_bytes[:].bitcast(I32), 0)
         nc.vector.memset(warm[:], 0.0)
-        nc.gpsimd.dma_start(out=size_col[:], in_=size.rearrange("o (p t) -> p (o t)", t=PACK))
-        make_identity(nc, ident[:])
-        nc.gpsimd.memset(placed[:], 0.0)
+        nc.vector.memset(placed[:], 0.0)
 
         def load_scale_rows(tile, scales):
             for r in range(4):
                 nc.sync.dma_start(out=tile[r:P:32, :].bitcast(I32), in_=scales[0, r:16:4, :].bitcast(I32))
 
-        nc.sync.dma_start(offsets[:], offs)
-        nc.scalar.dma_start(out=k_words[:].bitcast(I32), in_=keys_words[0].bitcast(I32))
-        load_scale_rows(k_bytes, keys_scales)
-        nc.scalar.dma_start(out=q_raw[:], in_=query.rearrange("(p j) q -> p j q", j=PACK))
-        nc.scalar.dma_start(out=v_words[:].bitcast(I32), in_=vals_words[0].bitcast(I32))
         nc.scalar.activation(warm_out[:], warm[:], ACT.Exp)
+        nc.gpsimd.dma_start(out=g_raw[:], in_=gout.rearrange("(p j) q -> p j q", j=PACK))
+        nc.sync.dma_start(offsets[:], offs)
+        nc.sync.dma_start(out=k_words[:].bitcast(I32), in_=keys_words[0].bitcast(I32))
+        load_scale_rows(k_bytes, keys_scales)
+        nc.sync.dma_start(out=q_raw[:], in_=query.rearrange("(p j) q -> p j q", j=PACK))
+        nc.sync.dma_start(out=v_words[:].bitcast(I32), in_=vals_words[0].bitcast(I32))
         load_scale_rows(v_bytes, vals_scales)
-        nc.sync.dma_start(out=g_raw[:], in_=gout.rearrange("(p j) q -> p j q", j=PACK))
-        nc.sync.dma_start(out=old_sb[:], in_=old)
-
-        size_ps = ps.tile([P, PACK, P], F32, name="size_ps")
-        for t in range(PACK):
-            nc.tensor.transpose(size_ps[:, t, :], size_col[:, t:t + 1].to_broadcast([P, P]), ident[:])
-        size_row = sb.tile([P, P, PACK], F32, name="size_row", align_bytes=64)
-        nc.scalar.copy(size_row[:], size_ps[:].rearrange("q t p -> q p t"))
-        size_flat = size_row[:].rearrange("q p t -> q (p t)")
 
         def product(raw, words, scale_bytes, name):
             grouped = sb.tile([P, Q, PACK], BF16, name=name + "_grouped", align_bytes=64)
@@ -90,13 +76,21 @@ def tile_attend_bshareofshare_s_kernel(tc, query, keys_words, keys_scales, gout,
 
         a = product(q_raw, k_words, k_bytes, "a")
 
+        size_row = sb.tile([P, I], F32, name="size_row", tag="k_bytes", align_bytes=64)
+        nc.sync.dma_start(out=size_row[:], in_=size.partition_broadcast(P))
+        size_flat = size_row[:]
+        old_lo = sb.tile([P, T // 2], F32, name="old_lo", tag="k_words", align_bytes=64)
+        nc.sync.dma_start(out=old_lo[:], in_=old[:, 0:T // 2])
+
         p = sb.tile([P, I], F32, name="p", align_bytes=64)
         p2 = sb.tile([P, I], F32, name="p2", align_bytes=64)
-        s2z = sb.tile([P, G + 1], F32, name="s2z", align_bytes=64)
+        z = sb.tile([P, 1], F32, name="z")
         nc.scalar.activation(p2[:], a[:], ACT.Exp, scale=2.0)
-        nc.scalar.activation(p[:], a[:], ACT.Exp, accum_out=s2z[:, G:G + 1])
+        nc.scalar.activation(p[:], a[:], ACT.Exp, accum_out=z[:])
 
         c0 = product(g_raw, v_words, v_bytes, "c")
+        old_hi = sb.tile([P, T // 2], F32, name="old_hi", tag="v_words", align_bytes=64)
+        nc.sync.dma_start(out=old_hi[:], in_=old[:, T // 2:T])
 
         def grp(ap):
             return ap.rearrange("q (g j) -> q g j", j=GS)
@@ -104,15 +98,18 @@ def tile_attend_bshareofshare_s_kernel(tc, query, keys_words, keys_scales, gout,
         def spread(ap, n):
             return ap.unsqueeze(2).to_broadcast([P, n, GS])
 
-        s1 = sb.tile([P, G], F32, name="s1", align_bytes=64)
-        nc.vector.tensor_reduce(s2z[:, 0:G], grp(p2[:]), AX.X, ALU.add)
-        nc.vector.tensor_reduce(s1[:], grp(p[:]), AX.X, ALU.add)
-        root = sb.tile([P, G + 1], F32, name="root", align_bytes=64)
-        inv = sb.tile([P, G + 1], F32, name="inv", align_bytes=64)
-        nc.scalar.activation(root[:], s2z[:], ACT.Abs_reciprocal_sqrt)
+        sums = sb.tile([P, 2 * G + 1], F32, name="sums", tag="v_bytes", align_bytes=64)
+        s2 = sums[:, 0:G]
+        s1 = sums[:, G:2 * G]
+        inv_z = sums[:, 2 * G:2 * G + 1]
+        nc.vector.tensor_reduce(s2, grp(p2[:]), AX.X, ALU.add)
+        nc.vector.tensor_reduce(s1, grp(p[:]), AX.X, ALU.add)
+        root = sb.tile([P, G], F32, name="root", align_bytes=64)
+        inv = sb.tile([P, G], F32, name="inv", align_bytes=64)
+        nc.scalar.activation(root[:], s2, ACT.Abs_reciprocal_sqrt)
         nc.scalar.activation(inv[:], root[:], ACT.Square)
-        inv_s2 = inv[:, 0:G]
-        inv_z = inv[:, G:G + 1]
+        nc.vector.reciprocal(inv_z, z[:])
+        inv_s2 = inv[:]
 
         w = sb.tile([P, I], F32, name="w", align_bytes=64)
         u = sb.tile([P, I], F32, name="u", align_bytes=64)
@@ -135,7 +132,7 @@ def tile_attend_bshareofshare_s_kernel(tc, query, keys_words, keys_scales, gout,
             nc.vector.tensor_tensor(w[:, c], c0[:, c], size_flat[:, c], ALU.mult)
         for c in cols:
             nc.vector.tensor_tensor(u[:, c], w[:, c], p2[:, c], ALU.mult)
-        nc.vector.scalar_tensor_tensor(sh[:], s1[:], inv_z, inv_s2, ALU.mult, ALU.mult)
+        nc.vector.scalar_tensor_tensor(sh[:], s1, inv_z, inv_s2, ALU.mult, ALU.mult)
         for c, g in zip(cols, grps):
             nc.vector.tensor_reduce(dsh[:, g], grp(u[:, c]), AX.X, ALU.add)
         nc.vector.tensor_tensor(grp(psh[:]), grp(p[:]), spread(sh[:], G), ALU.mult)
@@ -155,6 +152,8 @@ def tile_attend_bshareofshare_s_kernel(tc, query, keys_words, keys_scales, gout,
             c = slice(start, start + width)
             start = start + width
             res = sb.tile([P, width], F32, name="res%d" % n, align_bytes=64)
-            nc.vector.tensor_tensor(res[:], old_sb[:, c], placed[:, c], ALU.add)
+            old_half = old_lo if c.start < T // 2 else old_hi
+            lo = c.start % (T // 2)
+            nc.vector.tensor_tensor(res[:], old_half[:, lo:lo + width], placed[:, c], ALU.add)
             queue = nc.sync if n % 2 == 0 else nc.scalar
             queue.dma_start(out=out[:, c], in_=res[:])

@@ -1,6 +1,7 @@
 from contextlib import ExitStack
 
 import concourse.mybir as mybir
+from concourse.masks import make_identity
 
 D, E, T, I, Q, G = 512, 512, 2048, 512, 128, 64
 FLOPS = 2 * 2 * 512 * Q * I
@@ -21,22 +22,26 @@ P = 128
 PACK = 4
 GS = I // G
 HALVES = 2
-OUT_CHUNKS = (256, 768, 768, 256)
+OUT_CHUNKS = (256, 512, 512, 512, 256)
 
 
 def tile_attend_bshareofshare_s_kernel(tc, query, keys_words, keys_scales, gout, vals_words, vals_scales, size, old, offs, out):
     nc = tc.nc
     with ExitStack() as ctx:
         sb = ctx.enter_context(tc.tile_pool(name="sb", bufs=1))
+        after_q = ctx.enter_context(tc.tile_pool(name="after_q", bufs=1))
         ps = ctx.enter_context(tc.psum_pool(name="ps", bufs=1))
 
         offsets = sb.tile([P, I // 16], U16, name="offsets")
-        k_words = sb.tile([P, T], U16, name="k_words", tag="k_words", align_bytes=64)
+        k_words = sb.tile([P, T], U16, name="k_words", align_bytes=64)
         v_words = sb.tile([P, T], U16, name="v_words", tag="v_words", align_bytes=64)
-        k_bytes = sb.tile([P, T], U8, name="k_bytes", tag="k_bytes", align_bytes=64)
+        k_bytes = sb.tile([P, T], U8, name="k_bytes", align_bytes=64)
         v_bytes = sb.tile([P, T], U8, name="v_bytes", tag="v_bytes", align_bytes=64)
-        q_raw = sb.tile([P, PACK, Q], F32, name="q_raw", align_bytes=64)
-        g_raw = sb.tile([P, PACK, Q], F32, name="g_raw", align_bytes=64)
+        q_raw = sb.tile([P, PACK, Q], F32, name="q_raw", tag="c_grouped", align_bytes=64)
+        g_raw = sb.tile([P, PACK, Q], F32, name="g_raw", tag="g_raw", align_bytes=64)
+        old_sb = sb.tile([P, T], F32, name="old_sb", align_bytes=64)
+        size_col = after_q.tile([P, PACK], F32, name="size_col", offset=0, align_bytes=64)
+        ident = sb.tile([P, P], F32, name="ident", align_bytes=64)
         placed = sb.tile([P, T], F32, name="placed", align_bytes=64)
         warm = sb.tile([P, 1], F32, name="warm")
         warm_out = sb.tile([P, 1], F32, name="warm_out")
@@ -46,27 +51,36 @@ def tile_attend_bshareofshare_s_kernel(tc, query, keys_words, keys_scales, gout,
         nc.vector.memset(warm[:], 0.0)
         nc.vector.memset(placed[:], 0.0)
 
-        def load_scale_rows(tile, scales):
-            for r in range(4):
-                nc.sync.dma_start(out=tile[r:P:32, :].bitcast(I32), in_=scales[0, r:16:4, :].bitcast(I32))
+        make_identity(nc, ident[:])
 
+        def load_scale_rows(queue, tile, scales):
+            for r in range(4):
+                queue.dma_start(out=tile[r:P:32, :].bitcast(I32), in_=scales[0, r:16:4, :].bitcast(I32))
+
+        nc.scalar.dma_start(out=size_col[:], in_=size.rearrange("o (p t) -> p (o t)", t=PACK))
         nc.scalar.activation(warm_out[:], warm[:], ACT.Exp)
-        nc.gpsimd.dma_start(out=g_raw[:], in_=gout.rearrange("(p j) q -> p j q", j=PACK))
         nc.sync.dma_start(offsets[:], offs)
         nc.sync.dma_start(out=k_words[:].bitcast(I32), in_=keys_words[0].bitcast(I32))
-        load_scale_rows(k_bytes, keys_scales)
+        load_scale_rows(nc.sync, k_bytes, keys_scales)
         nc.sync.dma_start(out=q_raw[:], in_=query.rearrange("(p j) q -> p j q", j=PACK))
         nc.sync.dma_start(out=v_words[:].bitcast(I32), in_=vals_words[0].bitcast(I32))
-        load_scale_rows(v_bytes, vals_scales)
+        nc.sync.dma_start(out=g_raw[:], in_=gout.rearrange("(p j) q -> p j q", j=PACK))
+        load_scale_rows(nc.sync, v_bytes, vals_scales)
+        nc.sync.dma_start(out=old_sb[:], in_=old)
 
-        def product(raw, words, scale_bytes, name):
-            grouped = sb.tile([P, Q, PACK], BF16, name=name + "_grouped", align_bytes=64)
-            codes = sb.tile([P, Q], U32, name=name + "_codes", align_bytes=64)
-            scales = sb.tile([P, Q], U8, name=name + "_scales", align_bytes=64)
-            picked_words = sb.tile([P, I], U16, name=name + "_picked_words", align_bytes=64)
-            picked_bytes = sb.tile([P, I], U8, name=name + "_picked_bytes", align_bytes=64)
-            acc = ps.tile([P, I], F32, name=name + "_acc")
+        size_ps = ps.tile([P, PACK, P], F32, name="size_ps")
+        for t in range(PACK):
+            nc.tensor.transpose(size_ps[:, t, :], size_col[:, t:t + 1].to_broadcast([P, P]), ident[:])
+        size_row = sb.tile([P, P, PACK], F32, name="size_row", align_bytes=64)
+        nc.scalar.copy(size_row[:], size_ps[:].rearrange("q t p -> q p t"))
+        size_flat = size_row[:].rearrange("q p t -> q (p t)")
+
+        def interleave(grouped, raw):
             nc.scalar.copy(grouped[:], raw[:].rearrange("p j q -> p q j"))
+
+        def product(grouped, codes, words, picked_words, scale_bytes, picked_bytes, name):
+            scales = sb.tile([P, Q], U8, name=name + "_scales", align_bytes=64)
+            acc = ps.tile([P, I], F32, name=name + "_acc")
             nc.vector.tensor_copy(picked_words[:], words[:].indirect(offsets[:]))
             nc.vector.quantize_mx(out=codes[:].bitcast(FP8X4), scales=scales[:], in_=grouped[:].rearrange("p q j -> p (q j)"))
             nc.vector.tensor_copy(picked_bytes[:], scale_bytes[:].indirect(offsets[:]))
@@ -74,23 +88,25 @@ def tile_attend_bshareofshare_s_kernel(tc, query, keys_words, keys_scales, gout,
                                 rhs=picked_words[:].bitcast(FP4X4), rhs_scale=picked_bytes[:], start=True, stop=True)
             return acc
 
-        a = product(q_raw, k_words, k_bytes, "a")
-
-        size_row = sb.tile([P, I], F32, name="size_row", tag="k_bytes", align_bytes=64)
-        nc.sync.dma_start(out=size_row[:], in_=size.partition_broadcast(P))
-        size_flat = size_row[:]
-        old_lo = sb.tile([P, T // 2], F32, name="old_lo", tag="k_words", align_bytes=64)
-        nc.sync.dma_start(out=old_lo[:], in_=old[:, 0:T // 2])
+        q_grouped = after_q.tile([P, Q, PACK], BF16, name="q_grouped", offset=0, align_bytes=64)
+        g_grouped = sb.tile([P, Q, PACK], BF16, name="g_grouped", tag="c_grouped", align_bytes=64)
+        interleave(q_grouped, q_raw)
+        interleave(g_grouped, g_raw)
+        q_codes = sb.tile([P, Q], U32, name="q_codes", align_bytes=64)
+        k_picked_words = sb.tile([P, I], U16, name="k_picked_words", align_bytes=64)
+        k_picked_bytes = sb.tile([P, I], U8, name="k_picked_bytes", align_bytes=64)
+        a = product(q_grouped, q_codes, k_words, k_picked_words, k_bytes, k_picked_bytes, "a")
 
         p = sb.tile([P, I], F32, name="p", align_bytes=64)
-        p2 = sb.tile([P, I], F32, name="p2", align_bytes=64)
+        p2 = sb.tile([P, I], F32, name="p2", tag="g_raw", align_bytes=64)
         z = sb.tile([P, 1], F32, name="z")
         nc.scalar.activation(p2[:], a[:], ACT.Exp, scale=2.0)
         nc.scalar.activation(p[:], a[:], ACT.Exp, accum_out=z[:])
 
-        c0 = product(g_raw, v_words, v_bytes, "c")
-        old_hi = sb.tile([P, T // 2], F32, name="old_hi", tag="v_words", align_bytes=64)
-        nc.sync.dma_start(out=old_hi[:], in_=old[:, T // 2:T])
+        g_codes = sb.tile([P, Q], U32, name="g_codes", tag="v_words", align_bytes=64)
+        v_picked_bytes = after_q.tile([P, I], U8, name="v_picked_bytes", offset=0, align_bytes=64)
+        v_picked_words = after_q.tile([P, I], U16, name="v_picked_words", offset=I, align_bytes=64)
+        c0 = product(g_grouped, g_codes, v_words, v_picked_words, v_bytes, v_picked_bytes, "c")
 
         def grp(ap):
             return ap.rearrange("q (g j) -> q g j", j=GS)
@@ -98,10 +114,11 @@ def tile_attend_bshareofshare_s_kernel(tc, query, keys_words, keys_scales, gout,
         def spread(ap, n):
             return ap.unsqueeze(2).to_broadcast([P, n, GS])
 
-        sums = sb.tile([P, 2 * G + 1], F32, name="sums", tag="v_bytes", align_bytes=64)
-        s2 = sums[:, 0:G]
-        s1 = sums[:, G:2 * G]
-        inv_z = sums[:, 2 * G:2 * G + 1]
+        s2_t = sb.tile([P, G], F32, name="s2", tag="v_bytes", align_bytes=64)
+        sums = sb.tile([P, G + 1], F32, name="sums", tag="c_grouped", align_bytes=64)
+        s2 = s2_t[:]
+        s1 = sums[:, 0:G]
+        inv_z = sums[:, G:G + 1]
         nc.vector.tensor_reduce(s2, grp(p2[:]), AX.X, ALU.add)
         nc.vector.tensor_reduce(s1, grp(p[:]), AX.X, ALU.add)
         root = sb.tile([P, G], F32, name="root", align_bytes=64)
@@ -152,8 +169,6 @@ def tile_attend_bshareofshare_s_kernel(tc, query, keys_words, keys_scales, gout,
             c = slice(start, start + width)
             start = start + width
             res = sb.tile([P, width], F32, name="res%d" % n, align_bytes=64)
-            old_half = old_lo if c.start < T // 2 else old_hi
-            lo = c.start % (T // 2)
-            nc.vector.tensor_tensor(res[:], old_half[:, lo:lo + width], placed[:, c], ALU.add)
+            nc.vector.tensor_tensor(res[:], old_sb[:, c], placed[:, c], ALU.add)
             queue = nc.sync if n % 2 == 0 else nc.scalar
             queue.dma_start(out=out[:, c], in_=res[:])

@@ -21,7 +21,6 @@ AX = mybir.AxisListType
 P = 128
 PACK = 4
 GS = I // G
-HALVES = 2
 OUT_CHUNKS = (256, 512, 512, 512, 256)
 
 
@@ -29,6 +28,7 @@ def tile_attend_bshareofshare_s_kernel(tc, query, keys_words, keys_scales, gout,
     nc = tc.nc
     with ExitStack() as ctx:
         sb = ctx.enter_context(tc.tile_pool(name="sb", bufs=1))
+        after_v = ctx.enter_context(tc.tile_pool(name="after_v", bufs=1))
         after_q = ctx.enter_context(tc.tile_pool(name="after_q", bufs=1))
         ps = ctx.enter_context(tc.psum_pool(name="ps", bufs=1))
 
@@ -36,7 +36,7 @@ def tile_attend_bshareofshare_s_kernel(tc, query, keys_words, keys_scales, gout,
         k_words = sb.tile([P, T], U16, name="k_words", align_bytes=64)
         v_words = sb.tile([P, T], U16, name="v_words", tag="v_words", align_bytes=64)
         k_bytes = sb.tile([P, T], U8, name="k_bytes", align_bytes=64)
-        v_bytes = sb.tile([P, T], U8, name="v_bytes", tag="v_bytes", align_bytes=64)
+        v_bytes = after_v.tile([P, T], U8, name="v_bytes", offset=0, align_bytes=64)
         q_raw = sb.tile([P, PACK, Q], F32, name="q_raw", tag="c_grouped", align_bytes=64)
         g_raw = sb.tile([P, PACK, Q], F32, name="g_raw", tag="g_raw", align_bytes=64)
         old_sb = sb.tile([P, T], F32, name="old_sb", align_bytes=64)
@@ -111,58 +111,50 @@ def tile_attend_bshareofshare_s_kernel(tc, query, keys_words, keys_scales, gout,
         def grp(ap):
             return ap.rearrange("q (g j) -> q g j", j=GS)
 
-        def spread(ap, n):
-            return ap.unsqueeze(2).to_broadcast([P, n, GS])
+        def spread(ap):
+            return ap.unsqueeze(2).to_broadcast([P, G, GS])
 
-        s2_t = sb.tile([P, G], F32, name="s2", tag="v_bytes", align_bytes=64)
-        sums = sb.tile([P, G + 1], F32, name="sums", tag="c_grouped", align_bytes=64)
-        s2 = s2_t[:]
-        s1 = sums[:, 0:G]
-        inv_z = sums[:, G:G + 1]
-        nc.vector.tensor_reduce(s2, grp(p2[:]), AX.X, ALU.add)
-        nc.vector.tensor_reduce(s1, grp(p[:]), AX.X, ALU.add)
+        s2 = after_v.tile([P, G], F32, name="s2", offset=0, align_bytes=64)
+        sp2 = after_v.tile([P, I], F32, name="sp2", offset=4 * G, align_bytes=64)
+        s1 = sb.tile([P, G], F32, name="s1", tag="c_grouped", align_bytes=64)
+        nc.gpsimd.tensor_tensor(sp2[:], p2[:], size_flat, ALU.mult)
+        nc.vector.tensor_reduce(s2[:], grp(p2[:]), AX.X, ALU.add)
+        nc.vector.tensor_reduce(s1[:], grp(p[:]), AX.X, ALU.add)
         root = sb.tile([P, G], F32, name="root", align_bytes=64)
-        inv = sb.tile([P, G], F32, name="inv", align_bytes=64)
-        nc.scalar.activation(root[:], s2, ACT.Abs_reciprocal_sqrt)
-        nc.scalar.activation(inv[:], root[:], ACT.Square)
-        nc.vector.reciprocal(inv_z, z[:])
-        inv_s2 = inv[:]
+        root_z = sb.tile([P, 1], F32, name="root_z")
+        neg_root_z = sb.tile([P, 1], F32, name="neg_root_z")
+        neg_inv_z = sb.tile([P, 1], F32, name="neg_inv_z")
+        inv_s2 = sb.tile([P, G], F32, name="inv_s2", align_bytes=64)
+        coef = sb.tile([P, 2, G], F32, name="coef", align_bytes=64)
+        nc.scalar.activation(root_z[:], z[:], ACT.Abs_reciprocal_sqrt, scale=1.0 / 512.0)
+        nc.scalar.activation(root[:], s2[:], ACT.Abs_reciprocal_sqrt)
+        nc.scalar.activation(neg_root_z[:], root_z[:], ACT.Copy, scale=-1.0 / 512.0)
+        nc.scalar.activation(coef[:, 0, :], root[:], ACT.Square, scale=root_z[:])
+        nc.scalar.activation(inv_s2[:], root[:], ACT.Square)
+        nc.scalar.activation(neg_inv_z[:], neg_root_z[:], ACT.Copy, scale=root_z[:])
 
-        w = sb.tile([P, I], F32, name="w", align_bytes=64)
-        u = sb.tile([P, I], F32, name="u", align_bytes=64)
+        dsr = sb.tile([P, I], F32, name="dsr", align_bytes=64)
         dsh = sb.tile([P, G], F32, name="dsh", align_bytes=64)
         sh = sb.tile([P, G], F32, name="sh", align_bytes=64)
-        psh = sb.tile([P, I], F32, name="psh", align_bytes=64)
-        mean = sb.tile([P, G], F32, name="mean", align_bytes=64)
-        junk = sb.tile([P, G], F32, name="junk", align_bytes=64)
-        total = sb.tile([P, 1], F32, name="total")
-        lin = sb.tile([P, G], F32, name="lin", align_bytes=64)
-        y1 = sb.tile([P, I], F32, name="y1", align_bytes=64)
-        y2 = sb.tile([P, I], F32, name="y2", align_bytes=64)
+        ds = sb.tile([P, 2, G], F32, name="ds", align_bytes=64)
+        dz_terms = sb.tile([P, G], F32, name="dz_terms", align_bytes=64)
+        dz = sb.tile([P, 1], F32, name="dz")
+        t1 = sb.tile([P, I], F32, name="t1", align_bytes=64)
+        t2 = sb.tile([P, I], F32, name="t2", align_bytes=64)
+        t3 = sb.tile([P, I], F32, name="t3", align_bytes=64)
         y3 = sb.tile([P, I], F32, name="y3", align_bytes=64)
 
-        cols = [slice(h * I // HALVES, (h + 1) * I // HALVES) for h in range(HALVES)]
-        grps = [slice(h * G // HALVES, (h + 1) * G // HALVES) for h in range(HALVES)]
-        gh = G // HALVES
-
-        for c in cols:
-            nc.vector.tensor_tensor(w[:, c], c0[:, c], size_flat[:, c], ALU.mult)
-        for c in cols:
-            nc.vector.tensor_tensor(u[:, c], w[:, c], p2[:, c], ALU.mult)
-        nc.vector.scalar_tensor_tensor(sh[:], s1, inv_z, inv_s2, ALU.mult, ALU.mult)
-        for c, g in zip(cols, grps):
-            nc.vector.tensor_reduce(dsh[:, g], grp(u[:, c]), AX.X, ALU.add)
-        nc.vector.tensor_tensor(grp(psh[:]), grp(p[:]), spread(sh[:], G), ALU.mult)
-        nc.vector.tensor_tensor(mean[:], dsh[:], inv_s2, ALU.mult)
-        nc.vector.scalar_tensor_tensor(junk[:], dsh[:], -1.0, sh[:], ALU.mult, ALU.mult, accum_out=total[:])
-        for c, g in zip(cols, grps):
-            nc.vector.tensor_tensor(grp(y1[:, c]), grp(w[:, c]), spread(mean[:, g], gh), ALU.subtract)
-        nc.vector.tensor_scalar(lin[:], mean[:], total[:], inv_z, ALU.add, ALU.mult)
-        for c in cols:
-            nc.vector.scalar_tensor_tensor(y2[:, c], y1[:, c], 1024.0, psh[:, c], ALU.mult, ALU.mult)
-        for c, g in zip(cols, grps):
-            nc.vector.scalar_tensor_tensor(grp(y3[:, c]), spread(lin[:, g], gh), 512.0, grp(y2[:, c]), ALU.mult, ALU.add)
-        nc.vector.tensor_tensor(placed[:].indirect(offsets[:]), y3[:], p[:], ALU.mult)
+        nc.vector.tensor_tensor(dsr[:], c0[:], sp2[:], ALU.mult)
+        nc.vector.tensor_tensor(sh[:], s1[:], coef[:, 0, :], ALU.mult)
+        nc.vector.tensor_reduce(dsh[:], grp(dsr[:]), AX.X, ALU.add)
+        nc.vector.tensor_tensor(coef[:, 1, :], sh[:], inv_s2[:], ALU.mult)
+        nc.vector.scalar_tensor_tensor(grp(t1[:]), spread(sh[:]), 2.0, grp(dsr[:]), ALU.mult, ALU.mult)
+        nc.vector.tensor_tensor(ds[:], coef[:], dsh[:].unsqueeze(1).to_broadcast([P, 2, G]), ALU.mult)
+        nc.vector.scalar_tensor_tensor(dz_terms[:], dsh[:], neg_inv_z[:], sh[:], ALU.mult, ALU.mult, accum_out=dz[:])
+        nc.vector.scalar_tensor_tensor(grp(t3[:]), spread(ds[:, 1, :]), -2.0, grp(p2[:]), ALU.mult, ALU.mult)
+        nc.vector.scalar_tensor_tensor(grp(t2[:]), spread(ds[:, 0, :]), dz[:], grp(p[:]), ALU.add, ALU.mult)
+        nc.vector.tensor_tensor(y3[:], t1[:], t3[:], ALU.add)
+        nc.vector.tensor_tensor(placed[:].indirect(offsets[:]), y3[:], t2[:], ALU.add)
 
         start = 0
         for n, width in enumerate(OUT_CHUNKS):

from contextlib import ExitStack

import concourse.mybir as mybir
from concourse.masks import make_identity

D, E, T, I, Q, G = 512, 512, 2048, 512, 128, 64
FLOPS = 2 * 2 * 512 * Q * I

F32 = mybir.dt.float32
BF16 = mybir.dt.bfloat16
I32 = mybir.dt.int32
U32 = mybir.dt.uint32
U16 = mybir.dt.uint16
U8 = mybir.dt.uint8
FP8X4 = mybir.dt.float8_e4m3fn_x4
FP4X4 = mybir.dt.float4_e2m1fn_x4
ACT = mybir.ActivationFunctionType
ALU = mybir.AluOpType
AX = mybir.AxisListType

P = 128
PACK = 4
GS = I // G
OUT_CHUNKS = (256, 512, 512, 512, 256)


def tile_attend_bshareofshare_s_kernel(tc, query, keys_words, keys_scales, gout, vals_words, vals_scales, size, old, offs, out):
    nc = tc.nc
    with ExitStack() as ctx:
        sb = ctx.enter_context(tc.tile_pool(name="sb", bufs=1))
        after_v = ctx.enter_context(tc.tile_pool(name="after_v", bufs=1))
        after_q = ctx.enter_context(tc.tile_pool(name="after_q", bufs=1))
        ps = ctx.enter_context(tc.psum_pool(name="ps", bufs=1))

        offsets = sb.tile([P, I // 16], U16, name="offsets")
        k_words = sb.tile([P, T], U16, name="k_words", align_bytes=64)
        v_words = sb.tile([P, T], U16, name="v_words", tag="v_words", align_bytes=64)
        k_bytes = sb.tile([P, T], U8, name="k_bytes", align_bytes=64)
        v_bytes = after_v.tile([P, T], U8, name="v_bytes", offset=0, align_bytes=64)
        q_raw = sb.tile([P, PACK, Q], F32, name="q_raw", tag="c_grouped", align_bytes=64)
        g_raw = sb.tile([P, PACK, Q], F32, name="g_raw", tag="g_raw", align_bytes=64)
        old_sb = sb.tile([P, T], F32, name="old_sb", align_bytes=64)
        size_col = after_q.tile([P, PACK], F32, name="size_col", offset=0, align_bytes=64)
        ident = sb.tile([P, P], F32, name="ident", align_bytes=64)
        placed = sb.tile([P, T], F32, name="placed", align_bytes=64)
        warm = sb.tile([P, 1], F32, name="warm")
        warm_out = sb.tile([P, 1], F32, name="warm_out")

        nc.vector.memset(k_bytes[:].bitcast(I32), 0)
        nc.vector.memset(v_bytes[:].bitcast(I32), 0)
        nc.vector.memset(warm[:], 0.0)
        nc.vector.memset(placed[:], 0.0)

        make_identity(nc, ident[:])

        def load_scale_rows(queue, tile, scales):
            for r in range(4):
                queue.dma_start(out=tile[r:P:32, :].bitcast(I32), in_=scales[0, r:16:4, :].bitcast(I32))

        nc.scalar.dma_start(out=size_col[:], in_=size.rearrange("o (p t) -> p (o t)", t=PACK))
        nc.scalar.activation(warm_out[:], warm[:], ACT.Exp)
        nc.sync.dma_start(offsets[:], offs)
        nc.sync.dma_start(out=k_words[:].bitcast(I32), in_=keys_words[0].bitcast(I32))
        load_scale_rows(nc.sync, k_bytes, keys_scales)
        nc.sync.dma_start(out=q_raw[:], in_=query.rearrange("(p j) q -> p j q", j=PACK))
        nc.sync.dma_start(out=v_words[:].bitcast(I32), in_=vals_words[0].bitcast(I32))
        nc.sync.dma_start(out=g_raw[:], in_=gout.rearrange("(p j) q -> p j q", j=PACK))
        load_scale_rows(nc.sync, v_bytes, vals_scales)
        nc.sync.dma_start(out=old_sb[:], in_=old)

        size_ps = ps.tile([P, PACK, P], F32, name="size_ps")
        for t in range(PACK):
            nc.tensor.transpose(size_ps[:, t, :], size_col[:, t:t + 1].to_broadcast([P, P]), ident[:])
        size_row = sb.tile([P, P, PACK], F32, name="size_row", align_bytes=64)
        nc.scalar.copy(size_row[:], size_ps[:].rearrange("q t p -> q p t"))
        size_flat = size_row[:].rearrange("q p t -> q (p t)")

        def interleave(grouped, raw):
            nc.scalar.copy(grouped[:], raw[:].rearrange("p j q -> p q j"))

        def product(grouped, codes, words, picked_words, scale_bytes, picked_bytes, name):
            scales = sb.tile([P, Q], U8, name=name + "_scales", align_bytes=64)
            acc = ps.tile([P, I], F32, name=name + "_acc")
            nc.vector.tensor_copy(picked_words[:], words[:].indirect(offsets[:]))
            nc.vector.quantize_mx(out=codes[:].bitcast(FP8X4), scales=scales[:], in_=grouped[:].rearrange("p q j -> p (q j)"))
            nc.vector.tensor_copy(picked_bytes[:], scale_bytes[:].indirect(offsets[:]))
            nc.tensor.matmul_mx(out=acc[:], lhsT=codes[:].bitcast(FP8X4), lhsT_scale=scales[:],
                                rhs=picked_words[:].bitcast(FP4X4), rhs_scale=picked_bytes[:], start=True, stop=True)
            return acc

        q_grouped = after_q.tile([P, Q, PACK], BF16, name="q_grouped", offset=0, align_bytes=64)
        g_grouped = sb.tile([P, Q, PACK], BF16, name="g_grouped", tag="c_grouped", align_bytes=64)
        interleave(q_grouped, q_raw)
        interleave(g_grouped, g_raw)
        q_codes = sb.tile([P, Q], U32, name="q_codes", align_bytes=64)
        k_picked_words = sb.tile([P, I], U16, name="k_picked_words", align_bytes=64)
        k_picked_bytes = sb.tile([P, I], U8, name="k_picked_bytes", align_bytes=64)
        a = product(q_grouped, q_codes, k_words, k_picked_words, k_bytes, k_picked_bytes, "a")

        p = sb.tile([P, I], F32, name="p", align_bytes=64)
        p2 = sb.tile([P, I], F32, name="p2", tag="g_raw", align_bytes=64)
        z = sb.tile([P, 1], F32, name="z")
        nc.scalar.activation(p2[:], a[:], ACT.Exp, scale=2.0)
        nc.scalar.activation(p[:], a[:], ACT.Exp, accum_out=z[:])

        g_codes = sb.tile([P, Q], U32, name="g_codes", tag="v_words", align_bytes=64)
        v_picked_bytes = after_q.tile([P, I], U8, name="v_picked_bytes", offset=0, align_bytes=64)
        v_picked_words = after_q.tile([P, I], U16, name="v_picked_words", offset=I, align_bytes=64)
        c0 = product(g_grouped, g_codes, v_words, v_picked_words, v_bytes, v_picked_bytes, "c")

        def grp(ap):
            return ap.rearrange("q (g j) -> q g j", j=GS)

        def spread(ap):
            return ap.unsqueeze(2).to_broadcast([P, G, GS])

        s2 = after_v.tile([P, G], F32, name="s2", offset=0, align_bytes=64)
        sp2 = after_v.tile([P, I], F32, name="sp2", offset=4 * G, align_bytes=64)
        s1 = sb.tile([P, G], F32, name="s1", tag="c_grouped", align_bytes=64)
        nc.gpsimd.tensor_tensor(sp2[:], p2[:], size_flat, ALU.mult)
        nc.vector.tensor_reduce(s2[:], grp(p2[:]), AX.X, ALU.add)
        nc.vector.tensor_reduce(s1[:], grp(p[:]), AX.X, ALU.add)
        root = sb.tile([P, G], F32, name="root", align_bytes=64)
        root_z = sb.tile([P, 1], F32, name="root_z")
        neg_root_z = sb.tile([P, 1], F32, name="neg_root_z")
        neg_inv_z = sb.tile([P, 1], F32, name="neg_inv_z")
        inv_s2 = sb.tile([P, G], F32, name="inv_s2", align_bytes=64)
        coef = sb.tile([P, 2, G], F32, name="coef", align_bytes=64)
        nc.scalar.activation(root_z[:], z[:], ACT.Abs_reciprocal_sqrt, scale=1.0 / 512.0)
        nc.scalar.activation(root[:], s2[:], ACT.Abs_reciprocal_sqrt)
        nc.scalar.activation(neg_root_z[:], root_z[:], ACT.Copy, scale=-1.0 / 512.0)
        nc.scalar.activation(coef[:, 0, :], root[:], ACT.Square, scale=root_z[:])
        nc.scalar.activation(inv_s2[:], root[:], ACT.Square)
        nc.scalar.activation(neg_inv_z[:], neg_root_z[:], ACT.Copy, scale=root_z[:])

        dsr = sb.tile([P, I], F32, name="dsr", align_bytes=64)
        dsh = sb.tile([P, G], F32, name="dsh", align_bytes=64)
        sh = sb.tile([P, G], F32, name="sh", align_bytes=64)
        ds = sb.tile([P, 2, G], F32, name="ds", align_bytes=64)
        dz_terms = sb.tile([P, G], F32, name="dz_terms", align_bytes=64)
        dz = sb.tile([P, 1], F32, name="dz")
        t1 = sb.tile([P, I], F32, name="t1", align_bytes=64)
        t2 = sb.tile([P, I], F32, name="t2", align_bytes=64)
        t3 = sb.tile([P, I], F32, name="t3", align_bytes=64)
        y3 = sb.tile([P, I], F32, name="y3", align_bytes=64)

        nc.vector.tensor_tensor(dsr[:], c0[:], sp2[:], ALU.mult)
        nc.vector.tensor_tensor(sh[:], s1[:], coef[:, 0, :], ALU.mult)
        nc.vector.tensor_reduce(dsh[:], grp(dsr[:]), AX.X, ALU.add)
        nc.vector.tensor_tensor(coef[:, 1, :], sh[:], inv_s2[:], ALU.mult)
        nc.vector.scalar_tensor_tensor(grp(t1[:]), spread(sh[:]), 2.0, grp(dsr[:]), ALU.mult, ALU.mult)
        nc.vector.tensor_tensor(ds[:], coef[:], dsh[:].unsqueeze(1).to_broadcast([P, 2, G]), ALU.mult)
        nc.vector.scalar_tensor_tensor(dz_terms[:], dsh[:], neg_inv_z[:], sh[:], ALU.mult, ALU.mult, accum_out=dz[:])
        nc.vector.scalar_tensor_tensor(grp(t3[:]), spread(ds[:, 1, :]), -2.0, grp(p2[:]), ALU.mult, ALU.mult)
        nc.vector.scalar_tensor_tensor(grp(t2[:]), spread(ds[:, 0, :]), dz[:], grp(p[:]), ALU.add, ALU.mult)
        nc.vector.tensor_tensor(y3[:], t1[:], t3[:], ALU.add)
        nc.vector.tensor_tensor(placed[:].indirect(offsets[:]), y3[:], t2[:], ALU.add)

        start = 0
        for n, width in enumerate(OUT_CHUNKS):
            c = slice(start, start + width)
            start = start + width
            res = sb.tile([P, width], F32, name="res%d" % n, align_bytes=64)
            nc.vector.tensor_tensor(res[:], old_sb[:, c], placed[:, c], ALU.add)
            queue = nc.sync if n % 2 == 0 else nc.scalar
            queue.dma_start(out=out[:, c], in_=res[:])
